import numpy as np
import ml_dtypes


def mxq(x, axis, fmt="e4m3"):
    dtype, down = {"e4m3": (ml_dtypes.float8_e4m3fn, 7), "e5m2": (ml_dtypes.float8_e5m2, 14)}[fmt]
    v = np.moveaxis(np.asarray(x, np.float32).astype(ml_dtypes.bfloat16).astype(np.float64), axis, -1)
    blocks = v.reshape(v.shape[:-1] + (-1, 32))
    amax = np.abs(blocks).max(-1, keepdims=True)
    byte = np.maximum(np.where(amax > 0, np.frexp(amax)[1] - 1 + 127, 0) - down, 1)
    scale = np.exp2(byte - 127.0)
    codes = (blocks / scale).astype(np.float32).astype(dtype).astype(np.float64)
    return np.moveaxis((codes * scale).reshape(v.shape), -1, axis)


WIDE = False


def mx_kscale(k):
    if not WIDE:
        return np.ones(k)
    levels = np.array([10, -10, 5, -5, 0])
    if k % 512:
        return np.exp2(np.random.permutation(np.resize(levels, k // 32))).repeat(32)
    a = np.empty((k // 512, 16))
    for p in range(k // 512):
        a[p, :8] = np.random.permutation(np.resize(levels, 8))
        for g in range(8):
            far = levels[np.abs(levels - a[p, g]) >= 10]
            a[p, g + 8] = far[np.random.randint(len(far))]
    return np.exp2(a.ravel()).repeat(32)


def f64(x):
    return np.asarray(x).astype(np.float64)


def striped(idx):
    return np.tile(np.asarray(idx).reshape(-1, 16).T, (8, 1)).astype(np.uint16)


def unstriped(offs):
    return offs[:16].T.reshape(-1).astype(np.int64)


E2M1 = np.array([0.0, 0.5, 1.0, 1.5, 2.0, 3.0, 4.0, 6.0, -0.0, -0.5, -1.0, -1.5, -2.0, -3.0, -4.0, -6.0])


def pack_weight(w, fmt):
    k, n = w.shape
    w = f64(np.asarray(w, np.float32).astype(ml_dtypes.bfloat16)).reshape(k // 32, 32, n)
    amax = np.abs(w).max(1)
    if fmt == "e4m3":
        byte = np.frexp(amax)[1] - 1 + 127 - 7
    else:
        mant, ex = np.frexp(amax / 6.0)
        byte = np.where(mant > 0.5, ex, ex - 1) + 127
    byte = np.clip(np.where(amax > 0, byte, 1), 1, 254)
    scaled = (w * np.exp2(127.0 - byte)[:, None, :]).reshape(k, n).astype(np.float32)
    by_word = np.ascontiguousarray(scaled.reshape(k // 512, 128, 4, n).transpose(0, 1, 3, 2))
    if fmt == "e4m3":
        words = by_word.astype(ml_dtypes.float8_e4m3fn).view(np.uint8)
    else:
        c = by_word.astype(ml_dtypes.float4_e2m1fn).view(np.uint8) & 0xF
        words = (c[..., 0::2] | (c[..., 1::2] << 4)).reshape(k // 512, 128, 2 * n)
    return np.ascontiguousarray(words), np.ascontiguousarray(byte.astype(np.uint8).reshape(k // 512, 16, n))


def unpack_weight(words, scales, fmt):
    g, _, n = scales.shape
    words = np.ascontiguousarray(words).reshape(g, 128, n, -1)
    if fmt == "e4m3":
        vals = words.view(ml_dtypes.float8_e4m3fn).astype(np.float64)
    else:
        nib = np.empty((g, 128, n, 4), np.uint8)
        nib[..., 0::2] = words & 0xF
        nib[..., 1::2] = words >> 4
        vals = E2M1[nib]
    vals = vals * np.repeat(np.exp2(scales.astype(np.float64) - 127.0), 8, axis=1)[..., None]
    return vals.transpose(0, 1, 3, 2).reshape(g * 512, n)


K, T, J, N = 1024, 2048, 512, 512


def setup_inputs():
    n = np.random.standard_normal
    idx = np.random.permutation(T)[:J]
    fk = mx_kscale(K)
    xqp = pack_weight(n((K, T)) / fk[:, None], "e4m3")
    wbp = pack_weight(n((K, N)) * 1 / np.sqrt(K) * fk[:, None], "e2m1")
    return {
        "xq_words": xqp[0],
        "xq_scales": xqp[1],
        "wa": (n((K, N)) * 1 / np.sqrt(K) * fk[:, None]).astype(np.float32),
        "wb_words": wbp[0],
        "wb_scales": wbp[1],
        "offs": striped(idx),
    }


def reference(xq_words, xq_scales, wa, wb_words, wb_scales, offs):
    idx = unstriped(offs)
    xqu = unpack_weight(xq_words, xq_scales, "e4m3")
    wbu = unpack_weight(wb_words, wb_scales, "e2m1")
    waq = mxq(f64(wa), 0, "e4m3")
    xqidxg = xqu[:, idx]
    p = waq.T @ xqidxg
    q = wbu.T @ xqidxg
    y = p + np.tanh(p - q)
    return y

@@ -1,0 +1,173 @@
+from contextlib import ExitStack
+
+import concourse.mybir as mybir
+
+K, T, J, N = 1024, 2048, 512, 512
+FLOPS = 2 * 2 * K * N * J
+
+F32 = mybir.dt.float32
+BF16 = mybir.dt.bfloat16
+I32 = mybir.dt.int32
+U32 = mybir.dt.uint32
+U16 = mybir.dt.uint16
+U8 = mybir.dt.uint8
+FP8X4 = mybir.dt.float8_e4m3fn_x4
+FP4X4 = mybir.dt.float4_e2m1fn_x4
+ALU = mybir.AluOpType
+ACT = mybir.ActivationFunctionType
+
+P = 128
+PACK = 4
+PASSES = 2
+M = 128
+TILES = N // M
+
+
+def tile_list_expert_contrast_kernel(tc, xq_words, xq_scales, wa, wb_words, wb_scales, offs, out):
+    nc = tc.nc
+    with ExitStack() as ctx:
+        keep = ctx.enter_context(tc.tile_pool(name="keep", bufs=1))
+        psum = ctx.enter_context(tc.psum_pool(name="psum", bufs=1))
+
+        offsets = keep.tile([P, J // 16], U16, name="offsets")
+        xs_tab = keep.tile([P, PASSES * T], U8, name="xs_tab", align_bytes=64)
+        wb_s = keep.tile([P, PASSES * N], U8, name="wb_s", align_bytes=64)
+        wb_w = keep.tile([P, PASSES * 2 * N], U8, name="wb_w", align_bytes=64)
+        xw_tab = [keep.tile([P, T], I32, name=f"xw_tab{z}", align_bytes=64) for z in range(PASSES)]
+        xw = [keep.tile([P, J], U32, name=f"xw{z}", align_bytes=64) for z in range(PASSES)]
+        xs = [keep.tile([P, J], U8, name=f"xs{z}", align_bytes=64) for z in range(PASSES)]
+        warm = keep.tile([P, 1], F32, name="warm")
+        warm_out = keep.tile([P, 1], F32, name="warm_out")
+
+        def load_scale_rows(queue, plane, scales, quad):
+            queue.dma_start(
+                out=plane[32 * quad : 32 * quad + 4, :].bitcast(I32).rearrange("r (z c) -> r z c", z=PASSES),
+                in_=scales[:, 4 * quad : 4 * quad + 4, :].bitcast(I32).rearrange("z r c -> r z c"),
+            )
+
+        def load_wb_words():
+            nc.sync.dma_start(
+                out=wb_w[:].bitcast(I32).rearrange("p (z c) -> p z c", z=PASSES),
+                in_=wb_words.bitcast(I32).rearrange("z p c -> p z c"),
+            )
+
+        def load_x_words(z):
+            nc.sync.dma_start(out=xw_tab[z][:], in_=xq_words[z].rearrange("p c r -> p (c r)").bitcast(I32))
+
+        nc.vector.memset(xs_tab[:].bitcast(I32), 0)
+        nc.sync.dma_start(offsets[:], offs)
+        load_wb_words()
+        for quad in range(4):
+            load_scale_rows(nc.sync if quad == 0 else nc.scalar, xs_tab, xq_scales, quad)
+        nc.vector.memset(wb_s[:].bitcast(I32), 0)
+        nc.vector.memset(warm[:], 0.0)
+        for z in range(PASSES):
+            load_x_words(z)
+        for quad in range(4):
+            load_scale_rows(nc.scalar, wb_s, wb_scales, quad)
+        nc.scalar.activation(out=warm_out[:], in_=warm[:], func=ACT.Tanh)
+
+        raw = []
+        for c in range(TILES):
+            t = keep.tile([P, PASSES * PACK * M], F32, name=f"raw{c}", tag=f"raw{c}")
+            raw.append(t)
+            for z in range(PASSES):
+                nc.sync.dma_start(
+                    out=t[:, z * PACK * M : (z + 1) * PACK * M].rearrange("p (t n) -> p t n", t=PACK),
+                    in_=wa[z * 512 : (z + 1) * 512, c * M : (c + 1) * M].rearrange("(p t) n -> p t n", t=PACK),
+                )
+
+        for z in range(PASSES):
+            nc.vector.tensor_copy(xs[z][:], xs_tab[:, z * T : (z + 1) * T].indirect(offsets[:]))
+        for z in range(PASSES):
+            nc.vector.tensor_copy(xw[z][:], xw_tab[z][:].bitcast(U32).indirect(offsets[:]))
+
+        neg_p = [psum.tile([M, J], F32, name=f"neg_p{c}") for c in range(TILES)]
+        second = [psum.tile([M, J], F32, name=f"second{c}") for c in range(TILES)]
+        double = (2, 3)
+
+        def q_pass(c, z):
+            nc.tensor.matmul_mx(
+                out=second[c][:],
+                lhsT=wb_w[:, z * 2 * N + 2 * c * M : z * 2 * N + 2 * (c + 1) * M].bitcast(FP4X4),
+                lhsT_scale=wb_s[:, z * N + c * M : z * N + (c + 1) * M],
+                rhs=xw[z][:].bitcast(FP8X4),
+                rhs_scale=xs[z][:],
+                start=(z == 0),
+                stop=(z == PASSES - 1 and c not in double),
+            )
+
+        def p_pass(w, s, z, bank, start, stop):
+            nc.tensor.matmul_mx(
+                out=bank[:],
+                lhsT=w[:].bitcast(FP8X4),
+                lhsT_scale=s[:],
+                rhs=xw[z][:].bitcast(FP8X4),
+                rhs_scale=xs[z][:],
+                start=start,
+                stop=stop,
+            )
+
+        def front(c, z, engine):
+            g = keep.tile([P, M, PACK], BF16, name=f"grouped{c}_{z}", align_bytes=64)
+            rows = raw[c][:, z * PACK * M : (z + 1) * PACK * M]
+            dst = g[:].rearrange("p (c i) t -> p c t i", i=4)
+            src = rows.rearrange("p (t c i) -> p c t i", t=PACK, i=4)
+            if engine == "V":
+                nc.vector.tensor_scalar(out=dst, in0=src, scalar1=-1.0, scalar2=None, op0=ALU.mult)
+            elif engine == "G":
+                nc.gpsimd.tensor_scalar(
+                    out=g[:],
+                    in0=rows.rearrange("p (t n) -> p n t", t=PACK),
+                    scalar1=-1.0,
+                    scalar2=0.0,
+                    op0=ALU.mult,
+                    op1=ALU.add,
+                )
+            else:
+                nc.scalar.activation(out=dst, in_=src, func=ACT.Copy, scale=-1.0)
+            w = keep.tile([P, M], U32, name=f"wa_w{c}_{z}", align_bytes=64)
+            s = keep.tile([P, M], U8, name=f"wa_s{c}_{z}", align_bytes=64)
+            nc.vector.quantize_mx(out=w[:].bitcast(FP8X4), scales=s[:], in_=g[:].rearrange("p n t -> p (n t)"))
+            if c in double:
+                p_pass(w, s, z, second[c], False, z == PASSES - 1)
+            p_pass(w, s, z, neg_p[c], z == 0, z == PASSES - 1)
+
+        def back(c, parts):
+            th = keep.tile([M, J], F32, name=f"th{c}")
+            res = keep.tile([M, J], F32, name=f"res{c}")
+            if c in double:
+                src = second[c]
+            else:
+                q_cols = q_sb[:, c * J : (c + 1) * J]
+                nc.scalar.copy(out=q_cols, in_=second[c][:])
+                src = keep.tile([M, J], F32, name=f"diff{c}")
+                nc.vector.tensor_tensor(out=src[:], in0=neg_p[c][:], in1=q_cols, op=ALU.add)
+            w = J // parts
+            for h in range(parts):
+                cols = slice(h * w, (h + 1) * w)
+                nc.scalar.activation(out=th[:, cols], in_=src[:, cols], func=ACT.Tanh, scale=-1.0)
+                nc.vector.tensor_tensor(out=res[:, cols], in0=th[:, cols], in1=neg_p[c][:, cols], op=ALU.subtract)
+                nc.sync.dma_start(out=out[c * M : (c + 1) * M, cols], in_=res[:, cols])
+
+        cast_engine = "SSVSVSVS"
+
+        def fronts(c):
+            for z in range(PASSES):
+                front(c, z, cast_engine[PASSES * c + z])
+
+        for c in range(TILES):
+            q_pass(c, 0)
+        q_pass(0, 1)
+        q_pass(1, 1)
+        fronts(0)
+        q_sb = keep.tile([M, 2 * J], F32, name="q_sb", tag="raw0")
+        q_pass(2, 1)
+        q_pass(3, 1)
+        fronts(1)
+        fronts(2)
+        back(0, 1)
+        fronts(3)
+        back(1, 1)
+        back(2, 1)
+        back(3, 2)

@@ -33,7 +33,7 @@ def tile_list_expert_contrast_kernel(tc, xq_words, xq_scales, wa, wb_words, wb_s
         xs_tab = keep.tile([P, PASSES * T], U8, name="xs_tab", align_bytes=64)
         wb_s = keep.tile([P, PASSES * N], U8, name="wb_s", align_bytes=64)
         wb_w = keep.tile([P, PASSES * 2 * N], U8, name="wb_w", align_bytes=64)
-        xw_tab = [keep.tile([P, T], I32, name=f"xw_tab{z}", align_bytes=64) for z in range(PASSES)]
+        xw_tab = [keep.tile([P, T], I32, name=f"xw_tab{z}", tag=f"xw_tab{z}", align_bytes=64) for z in range(PASSES)]
         xw = [keep.tile([P, J], U32, name=f"xw{z}", align_bytes=64) for z in range(PASSES)]
         xs = [keep.tile([P, J], U8, name=f"xs{z}", align_bytes=64) for z in range(PASSES)]
         warm = keep.tile([P, 1], F32, name="warm")
@@ -56,16 +56,16 @@ def tile_list_expert_contrast_kernel(tc, xq_words, xq_scales, wa, wb_words, wb_s
 
         nc.vector.memset(xs_tab[:].bitcast(I32), 0)
         nc.sync.dma_start(offsets[:], offs)
-        load_wb_words()
         for quad in range(4):
-            load_scale_rows(nc.sync if quad == 0 else nc.scalar, xs_tab, xq_scales, quad)
-        nc.vector.memset(wb_s[:].bitcast(I32), 0)
+            load_scale_rows(nc.sync if quad < 2 else nc.scalar, xs_tab, xq_scales, quad)
         nc.vector.memset(warm[:], 0.0)
+        nc.vector.memset(wb_s[:].bitcast(I32), 0)
+        load_wb_words()
         for z in range(PASSES):
             load_x_words(z)
+        nc.scalar.activation(out=warm_out[:], in_=warm[:], func=ACT.Tanh)
         for quad in range(4):
             load_scale_rows(nc.scalar, wb_s, wb_scales, quad)
-        nc.scalar.activation(out=warm_out[:], in_=warm[:], func=ACT.Tanh)
 
         raw = []
         for c in range(TILES):
@@ -100,24 +100,23 @@ def tile_list_expert_contrast_kernel(tc, xq_words, xq_scales, wa, wb_words, wb_s
         def p_pass(w, s, z, bank, start, stop):
             nc.tensor.matmul_mx(
                 out=bank[:],
-                lhsT=w[:].bitcast(FP8X4),
-                lhsT_scale=s[:],
+                lhsT=w.bitcast(FP8X4),
+                lhsT_scale=s,
                 rhs=xw[z][:].bitcast(FP8X4),
                 rhs_scale=xs[z][:],
                 start=start,
                 stop=stop,
             )
 
-        def front(c, z, engine):
-            g = keep.tile([P, M, PACK], BF16, name=f"grouped{c}_{z}", align_bytes=64)
+        def cast(c, z, engine, g):
             rows = raw[c][:, z * PACK * M : (z + 1) * PACK * M]
-            dst = g[:].rearrange("p (c i) t -> p c t i", i=4)
+            dst = g.rearrange("p (c i t) -> p c t i", i=4, t=PACK)
             src = rows.rearrange("p (t c i) -> p c t i", t=PACK, i=4)
             if engine == "V":
                 nc.vector.tensor_scalar(out=dst, in0=src, scalar1=-1.0, scalar2=None, op0=ALU.mult)
             elif engine == "G":
                 nc.gpsimd.tensor_scalar(
-                    out=g[:],
+                    out=g.rearrange("p (n t) -> p n t", t=PACK),
                     in0=rows.rearrange("p (t n) -> p n t", t=PACK),
                     scalar1=-1.0,
                     scalar2=0.0,
@@ -126,12 +125,29 @@ def tile_list_expert_contrast_kernel(tc, xq_words, xq_scales, wa, wb_words, wb_s
                 )
             else:
                 nc.scalar.activation(out=dst, in_=src, func=ACT.Copy, scale=-1.0)
-            w = keep.tile([P, M], U32, name=f"wa_w{c}_{z}", align_bytes=64)
-            s = keep.tile([P, M], U8, name=f"wa_s{c}_{z}", align_bytes=64)
-            nc.vector.quantize_mx(out=w[:].bitcast(FP8X4), scales=s[:], in_=g[:].rearrange("p n t -> p (n t)"))
+
+        def p_passes(c, z, w, s):
             if c in double:
                 p_pass(w, s, z, second[c], False, z == PASSES - 1)
             p_pass(w, s, z, neg_p[c], z == 0, z == PASSES - 1)
+
+        def front(c, z, engine):
+            g = keep.tile([P, M * PACK], BF16, name=f"grouped{c}_{z}", align_bytes=64)
+            cast(c, z, engine, g[:])
+            w = keep.tile([P, M], U32, name=f"wa_w{c}_{z}", align_bytes=64)
+            s = keep.tile([P, M], U8, name=f"wa_s{c}_{z}", align_bytes=64)
+            nc.vector.quantize_mx(out=w[:].bitcast(FP8X4), scales=s[:], in_=g[:])
+            p_passes(c, z, w[:], s[:])
+
+        def first_fronts():
+            g = keep.tile([P, PASSES * M * PACK], BF16, name="grouped0", align_bytes=64)
+            for z in range(PASSES):
+                cast(0, z, cast_engine[z], g[:, z * M * PACK : (z + 1) * M * PACK])
+            w = keep.tile([P, PASSES * M], U32, name="wa_w0", tag="xw_tab1", align_bytes=64)
+            s = keep.tile([P, PASSES * M], U8, name="wa_s0", align_bytes=64)
+            nc.vector.quantize_mx(out=w[:].bitcast(FP8X4), scales=s[:], in_=g[:])
+            for z in range(PASSES):
+                p_passes(0, z, w[:, z * M : (z + 1) * M], s[:, z * M : (z + 1) * M])
 
         def back(c, parts):
             th = keep.tile([M, J], F32, name=f"th{c}")
@@ -150,7 +166,7 @@ def tile_list_expert_contrast_kernel(tc, xq_words, xq_scales, wa, wb_words, wb_s
                 nc.vector.tensor_tensor(out=res[:, cols], in0=th[:, cols], in1=neg_p[c][:, cols], op=ALU.subtract)
                 nc.sync.dma_start(out=out[c * M : (c + 1) * M, cols], in_=res[:, cols])
 
-        cast_engine = "SSVSVSVS"
+        cast_engine = "SSSSSVSV"
 
         def fronts(c):
             for z in range(PASSES):
@@ -160,14 +176,12 @@ def tile_list_expert_contrast_kernel(tc, xq_words, xq_scales, wa, wb_words, wb_s
             q_pass(c, 0)
         q_pass(0, 1)
         q_pass(1, 1)
-        fronts(0)
-        q_sb = keep.tile([M, 2 * J], F32, name="q_sb", tag="raw0")
+        first_fronts()
         q_pass(2, 1)
         q_pass(3, 1)
-        fronts(1)
-        fronts(2)
-        back(0, 1)
-        fronts(3)
-        back(1, 1)
-        back(2, 1)
+        for c in range(1, TILES):
+            fronts(c)
+        q_sb = keep.tile([M, 2 * J], F32, name="q_sb", tag="raw1")
+        for c in range(TILES - 1):
+            back(c, 1)
         back(3, 2)

@@ -35,7 +35,9 @@ def tile_list_expert_contrast_kernel(tc, xq_words, xq_scales, wa, wb_words, wb_s
         wb_w = keep.tile([P, PASSES * 2 * N], U8, name="wb_w", align_bytes=64)
         xw_tab = [keep.tile([P, T], I32, name=f"xw_tab{z}", tag=f"xw_tab{z}", align_bytes=64) for z in range(PASSES)]
         xw = [keep.tile([P, J], U32, name=f"xw{z}", align_bytes=64) for z in range(PASSES)]
-        xs = [keep.tile([P, J], U8, name=f"xs{z}", align_bytes=64) for z in range(PASSES)]
+        xs_picked = keep.tile([P, PASSES * J], U8, name="xs_picked", align_bytes=64)
+        xs_plane = keep.tile([P, PASSES * J], U8, name="xs_plane", align_bytes=64)
+        xs = [xs_plane[:, z * J : (z + 1) * J] for z in range(PASSES)]
         warm = keep.tile([P, 1], F32, name="warm")
         warm_out = keep.tile([P, 1], F32, name="warm_out")
 
@@ -54,33 +56,50 @@ def tile_list_expert_contrast_kernel(tc, xq_words, xq_scales, wa, wb_words, wb_s
         def load_x_words(z):
             nc.sync.dma_start(out=xw_tab[z][:], in_=xq_words[z].rearrange("p c r -> p (c r)").bitcast(I32))
 
-        nc.vector.memset(xs_tab[:].bitcast(I32), 0)
-        nc.sync.dma_start(offsets[:], offs)
-        for quad in range(4):
-            load_scale_rows(nc.sync if quad < 2 else nc.scalar, xs_tab, xq_scales, quad)
-        nc.vector.memset(warm[:], 0.0)
+        xs_words = xs_tab[:].bitcast(I32)
+        nc.vector.memset(xs_words[:, 0 : T // 4], 0)
+        nc.gpsimd.memset(xs_words[:, T // 4 : T // 2], 0)
         nc.vector.memset(wb_s[:].bitcast(I32), 0)
+        nc.vector.memset(warm[:], 0.0)
+        nc.vector.memset(xs_plane[:].bitcast(I32), 0)
+        nc.sync.dma_start(offsets[:], offs)
+        nc.sync.dma_start(
+            out=xs_tab[0:P:8, :].bitcast(I32).rearrange("r (z c) -> r z c", z=PASSES),
+            in_=xq_scales.bitcast(I32).rearrange("z r c -> r z c"),
+        )
         load_wb_words()
         for z in range(PASSES):
             load_x_words(z)
-        nc.scalar.activation(out=warm_out[:], in_=warm[:], func=ACT.Tanh)
         for quad in range(4):
             load_scale_rows(nc.scalar, wb_s, wb_scales, quad)
+        nc.scalar.activation(out=warm_out[:], in_=warm[:], func=ACT.Tanh)
 
-        raw = []
-        for c in range(TILES):
-            t = keep.tile([P, PASSES * PACK * M], F32, name=f"raw{c}", tag=f"raw{c}")
-            raw.append(t)
-            for z in range(PASSES):
-                nc.sync.dma_start(
-                    out=t[:, z * PACK * M : (z + 1) * PACK * M].rearrange("p (t n) -> p t n", t=PACK),
-                    in_=wa[z * 512 : (z + 1) * 512, c * M : (c + 1) * M].rearrange("(p t) n -> p t n", t=PACK),
-                )
+        raw = [keep.tile([P, PASSES * PACK * M], F32, name=f"raw{c}", tag=f"raw{c}") for c in range(TILES)]
+
+        def load_wa(c, z):
+            nc.sync.dma_start(
+                out=raw[c][:, z * PACK * M : (z + 1) * PACK * M].rearrange("p (t n) -> p t n", t=PACK),
+                in_=wa[z * 512 : (z + 1) * 512, c * M : (c + 1) * M].rearrange("(p t) n -> p t n", t=PACK),
+            )
 
         for z in range(PASSES):
-            nc.vector.tensor_copy(xs[z][:], xs_tab[:, z * T : (z + 1) * T].indirect(offsets[:]))
+            nc.vector.tensor_copy(
+                xs_picked[:, z * J : (z + 1) * J], xs_tab[:, z * T : (z + 1) * T].indirect(offsets[:])
+            )
         for z in range(PASSES):
             nc.vector.tensor_copy(xw[z][:], xw_tab[z][:].bitcast(U32).indirect(offsets[:]))
+
+        load_wa(0, 0)
+        for quad in range(4):
+            queue = nc.sync if quad < 2 else nc.scalar
+            queue.dma_start(
+                out=xs_plane[32 * quad : 32 * quad + 4, :].bitcast(I32),
+                in_=xs_picked[32 * quad : 32 * quad + 32 : 8, :].bitcast(I32),
+            )
+        for c in range(TILES):
+            for z in range(PASSES):
+                if (c, z) != (0, 0):
+                    load_wa(c, z)
 
         neg_p = [psum.tile([M, J], F32, name=f"neg_p{c}") for c in range(TILES)]
         second = [psum.tile([M, J], F32, name=f"second{c}") for c in range(TILES)]
@@ -92,7 +111,7 @@ def tile_list_expert_contrast_kernel(tc, xq_words, xq_scales, wa, wb_words, wb_s
                 lhsT=wb_w[:, z * 2 * N + 2 * c * M : z * 2 * N + 2 * (c + 1) * M].bitcast(FP4X4),
                 lhsT_scale=wb_s[:, z * N + c * M : z * N + (c + 1) * M],
                 rhs=xw[z][:].bitcast(FP8X4),
-                rhs_scale=xs[z][:],
+                rhs_scale=xs[z],
                 start=(z == 0),
                 stop=(z == PASSES - 1 and c not in double),
             )
@@ -103,7 +122,7 @@ def tile_list_expert_contrast_kernel(tc, xq_words, xq_scales, wa, wb_words, wb_s
                 lhsT=w.bitcast(FP8X4),
                 lhsT_scale=s,
                 rhs=xw[z][:].bitcast(FP8X4),
-                rhs_scale=xs[z][:],
+                rhs_scale=xs[z],
                 start=start,
                 stop=stop,
             )
@@ -139,16 +158,6 @@ def tile_list_expert_contrast_kernel(tc, xq_words, xq_scales, wa, wb_words, wb_s
             nc.vector.quantize_mx(out=w[:].bitcast(FP8X4), scales=s[:], in_=g[:])
             p_passes(c, z, w[:], s[:])
 
-        def first_fronts():
-            g = keep.tile([P, PASSES * M * PACK], BF16, name="grouped0", align_bytes=64)
-            for z in range(PASSES):
-                cast(0, z, cast_engine[z], g[:, z * M * PACK : (z + 1) * M * PACK])
-            w = keep.tile([P, PASSES * M], U32, name="wa_w0", tag="xw_tab1", align_bytes=64)
-            s = keep.tile([P, PASSES * M], U8, name="wa_s0", align_bytes=64)
-            nc.vector.quantize_mx(out=w[:].bitcast(FP8X4), scales=s[:], in_=g[:])
-            for z in range(PASSES):
-                p_passes(0, z, w[:, z * M : (z + 1) * M], s[:, z * M : (z + 1) * M])
-
         def back(c, parts):
             th = keep.tile([M, J], F32, name=f"th{c}")
             res = keep.tile([M, J], F32, name=f"res{c}")
@@ -176,7 +185,7 @@ def tile_list_expert_contrast_kernel(tc, xq_words, xq_scales, wa, wb_words, wb_s
             q_pass(c, 0)
         q_pass(0, 1)
         q_pass(1, 1)
-        first_fronts()
+        fronts(0)
         q_pass(2, 1)
         q_pass(3, 1)
         for c in range(1, TILES):

@@ -18,9 +18,16 @@ ACT = mybir.ActivationFunctionType
 
 P = 128
 PACK = 4
-PASSES = 2
+K_PASS = P * PACK
+PASSES = K // K_PASS
 M = 128
 TILES = N // M
+PIECE = PACK * M
+QUADS = 4
+SPREAD = 8
+RUN = 2
+SUMMED_IN_PSUM = range(TILES // 2, TILES)
+LAST = TILES - 1
 
 
 def tile_list_expert_contrast_kernel(tc, xq_words, xq_scales, wa, wb_words, wb_scales, offs, out):
@@ -30,167 +37,119 @@ def tile_list_expert_contrast_kernel(tc, xq_words, xq_scales, wa, wb_words, wb_s
         psum = ctx.enter_context(tc.psum_pool(name="psum", bufs=1))
 
         offsets = keep.tile([P, J // 16], U16, name="offsets")
-        xs_tab = keep.tile([P, PASSES * T], U8, name="xs_tab", align_bytes=64)
-        wb_s = keep.tile([P, PASSES * N], U8, name="wb_s", align_bytes=64)
-        wb_w = keep.tile([P, PASSES * 2 * N], U8, name="wb_w", align_bytes=64)
-        xw_tab = [keep.tile([P, T], I32, name=f"xw_tab{z}", tag=f"xw_tab{z}", align_bytes=64) for z in range(PASSES)]
-        xw = [keep.tile([P, J], U32, name=f"xw{z}", align_bytes=64) for z in range(PASSES)]
-        xs_picked = keep.tile([P, PASSES * J], U8, name="xs_picked", align_bytes=64)
-        xs_plane = keep.tile([P, PASSES * J], U8, name="xs_plane", align_bytes=64)
-        xs = [xs_plane[:, z * J : (z + 1) * J] for z in range(PASSES)]
-        warm = keep.tile([P, 1], F32, name="warm")
-        warm_out = keep.tile([P, 1], F32, name="warm_out")
+        x_scale_table = keep.tile([P, PASSES * T], U8, name="x_scale_table", align_bytes=64)
+        x_scale_picked = keep.tile([P, PASSES * J], U8, name="x_scale_picked", align_bytes=64)
+        x_planes = keep.tile([P, PASSES * J], U8, name="x_planes", align_bytes=64)
+        x_tables = [keep.tile([P, T], I32, name=f"x_table{z}", align_bytes=64) for z in range(PASSES)]
+        x_words = [keep.tile([P, J], U32, name=f"x_words{z}", align_bytes=64) for z in range(PASSES)]
+        wb_codes = keep.tile([P, PASSES * 2 * N], U8, name="wb_codes", align_bytes=64)
+        wb_planes = keep.tile([P, PASSES * N], U8, name="wb_planes", align_bytes=64)
+        wa_rows = [keep.tile([P, PASSES * PIECE], F32, name=f"wa_rows{c}") for c in range(TILES)]
 
-        def load_scale_rows(queue, plane, scales, quad):
-            queue.dma_start(
-                out=plane[32 * quad : 32 * quad + 4, :].bitcast(I32).rearrange("r (z c) -> r z c", z=PASSES),
-                in_=scales[:, 4 * quad : 4 * quad + 4, :].bitcast(I32).rearrange("z r c -> r z c"),
-            )
+        table_words = x_scale_table[:].bitcast(I32)
+        nc.vector.memset(table_words[:, 0 : T // 4], 0)
+        nc.gpsimd.memset(table_words[:, T // 4 : T // 2], 0)
+        nc.vector.memset(wb_planes[:].bitcast(I32), 0)
+        nc.vector.memset(x_planes[:].bitcast(I32), 0)
 
-        def load_wb_words():
-            nc.sync.dma_start(
-                out=wb_w[:].bitcast(I32).rearrange("p (z c) -> p z c", z=PASSES),
-                in_=wb_words.bitcast(I32).rearrange("z p c -> p z c"),
-            )
-
-        def load_x_words(z):
-            nc.sync.dma_start(out=xw_tab[z][:], in_=xq_words[z].rearrange("p c r -> p (c r)").bitcast(I32))
-
-        xs_words = xs_tab[:].bitcast(I32)
-        nc.vector.memset(xs_words[:, 0 : T // 4], 0)
-        nc.gpsimd.memset(xs_words[:, T // 4 : T // 2], 0)
-        nc.vector.memset(wb_s[:].bitcast(I32), 0)
-        nc.vector.memset(warm[:], 0.0)
-        nc.vector.memset(xs_plane[:].bitcast(I32), 0)
         nc.sync.dma_start(offsets[:], offs)
         nc.sync.dma_start(
-            out=xs_tab[0:P:8, :].bitcast(I32).rearrange("r (z c) -> r z c", z=PASSES),
-            in_=xq_scales.bitcast(I32).rearrange("z r c -> r z c"),
+            out=x_scale_table[0:P:SPREAD, :].bitcast(I32).rearrange("b (z c) -> b z c", z=PASSES),
+            in_=xq_scales.bitcast(I32).rearrange("z b c -> b z c"),
         )
-        load_wb_words()
+        nc.sync.dma_start(
+            out=wb_codes[:].bitcast(I32).rearrange("p (z c) -> p z c", z=PASSES),
+            in_=wb_words.bitcast(I32).rearrange("z p c -> p z c"),
+        )
         for z in range(PASSES):
-            load_x_words(z)
-        for quad in range(4):
-            load_scale_rows(nc.scalar, wb_s, wb_scales, quad)
-        nc.scalar.activation(out=warm_out[:], in_=warm[:], func=ACT.Tanh)
-
-        raw = [keep.tile([P, PASSES * PACK * M], F32, name=f"raw{c}", tag=f"raw{c}") for c in range(TILES)]
-
-        def load_wa(c, z):
-            nc.sync.dma_start(
-                out=raw[c][:, z * PACK * M : (z + 1) * PACK * M].rearrange("p (t n) -> p t n", t=PACK),
-                in_=wa[z * 512 : (z + 1) * 512, c * M : (c + 1) * M].rearrange("(p t) n -> p t n", t=PACK),
+            nc.sync.dma_start(out=x_tables[z][:], in_=xq_words[z].rearrange("p c r -> p (c r)").bitcast(I32))
+        for quad in range(QUADS):
+            nc.scalar.dma_start(
+                out=wb_planes[32 * quad : 32 * quad + 4, :].bitcast(I32).rearrange("r (z c) -> r z c", z=PASSES),
+                in_=wb_scales[:, 4 * quad : 4 * quad + 4, :].bitcast(I32).rearrange("z r c -> r z c"),
             )
 
         for z in range(PASSES):
             nc.vector.tensor_copy(
-                xs_picked[:, z * J : (z + 1) * J], xs_tab[:, z * T : (z + 1) * T].indirect(offsets[:])
+                x_scale_picked[:, z * J : (z + 1) * J], x_scale_table[:, z * T : (z + 1) * T].indirect(offsets[:])
             )
         for z in range(PASSES):
-            nc.vector.tensor_copy(xw[z][:], xw_tab[z][:].bitcast(U32).indirect(offsets[:]))
+            nc.vector.tensor_copy(x_words[z][:], x_tables[z][:].bitcast(U32).indirect(offsets[:]))
 
-        load_wa(0, 0)
-        for quad in range(4):
-            queue = nc.sync if quad < 2 else nc.scalar
-            queue.dma_start(
-                out=xs_plane[32 * quad : 32 * quad + 4, :].bitcast(I32),
-                in_=xs_picked[32 * quad : 32 * quad + 32 : 8, :].bitcast(I32),
+        def load_wa(c, z):
+            nc.sync.dma_start(
+                out=wa_rows[c][:, z * PIECE : (z + 1) * PIECE].rearrange("p (t n) -> p t n", t=PACK),
+                in_=wa[z * K_PASS : (z + 1) * K_PASS, c * M : (c + 1) * M].rearrange("(p t) n -> p t n", t=PACK),
             )
-        for c in range(TILES):
-            for z in range(PASSES):
-                if (c, z) != (0, 0):
-                    load_wa(c, z)
+
+        wa_pieces = [(c, z) for c in range(TILES) for z in range(PASSES)]
+        load_wa(*wa_pieces[0])
+        for quad in range(QUADS):
+            queue = nc.sync if quad < QUADS // 2 else nc.scalar
+            queue.dma_start(
+                out=x_planes[32 * quad : 32 * quad + 4, :].bitcast(I32),
+                in_=x_scale_picked[32 * quad : 32 * quad + 32 : SPREAD, :].bitcast(I32),
+            )
+        for c, z in wa_pieces[1:]:
+            load_wa(c, z)
 
         neg_p = [psum.tile([M, J], F32, name=f"neg_p{c}") for c in range(TILES)]
-        second = [psum.tile([M, J], F32, name=f"second{c}") for c in range(TILES)]
-        double = (2, 3)
+        q_bank = [psum.tile([M, J], F32, name=f"q_bank{c}") for c in range(TILES)]
 
-        def q_pass(c, z):
-            nc.tensor.matmul_mx(
-                out=second[c][:],
-                lhsT=wb_w[:, z * 2 * N + 2 * c * M : z * 2 * N + 2 * (c + 1) * M].bitcast(FP4X4),
-                lhsT_scale=wb_s[:, z * N + c * M : z * N + (c + 1) * M],
-                rhs=xw[z][:].bitcast(FP8X4),
-                rhs_scale=xs[z],
-                start=(z == 0),
-                stop=(z == PASSES - 1 and c not in double),
-            )
-
-        def p_pass(w, s, z, bank, start, stop):
+        def against_x(bank, z, codes, plane, start, stop):
             nc.tensor.matmul_mx(
                 out=bank[:],
-                lhsT=w.bitcast(FP8X4),
-                lhsT_scale=s,
-                rhs=xw[z][:].bitcast(FP8X4),
-                rhs_scale=xs[z],
+                lhsT=codes,
+                lhsT_scale=plane,
+                rhs=x_words[z][:].bitcast(FP8X4),
+                rhs_scale=x_planes[:, z * J : (z + 1) * J],
                 start=start,
                 stop=stop,
             )
 
-        def cast(c, z, engine, g):
-            rows = raw[c][:, z * PACK * M : (z + 1) * PACK * M]
-            dst = g.rearrange("p (c i t) -> p c t i", i=4, t=PACK)
-            src = rows.rearrange("p (t c i) -> p c t i", t=PACK, i=4)
-            if engine == "V":
-                nc.vector.tensor_scalar(out=dst, in0=src, scalar1=-1.0, scalar2=None, op0=ALU.mult)
-            elif engine == "G":
-                nc.gpsimd.tensor_scalar(
-                    out=g.rearrange("p (n t) -> p n t", t=PACK),
-                    in0=rows.rearrange("p (t n) -> p n t", t=PACK),
-                    scalar1=-1.0,
-                    scalar2=0.0,
-                    op0=ALU.mult,
-                    op1=ALU.add,
-                )
-            else:
+        def q_pass(c, z):
+            first = z * N + c * M
+            closes = z == PASSES - 1 and c not in SUMMED_IN_PSUM
+            codes = wb_codes[:, 2 * first : 2 * (first + M)].bitcast(FP4X4)
+            against_x(q_bank[c], z, codes, wb_planes[:, first : first + M], z == 0, closes)
+
+        def p_pass(c, z):
+            grouped = keep.tile([P, PIECE], BF16, name=f"grouped{c}_{z}", tag=f"grouped{c}_{z}", align_bytes=64)
+            src = wa_rows[c][:, z * PIECE : (z + 1) * PIECE].rearrange("p (t g i) -> p g t i", t=PACK, i=RUN)
+            dst = grouped[:].rearrange("p (g i t) -> p g t i", i=RUN, t=PACK)
+            if c == 0 or (c, z) == (LAST, 0):
                 nc.scalar.activation(out=dst, in_=src, func=ACT.Copy, scale=-1.0)
-
-        def p_passes(c, z, w, s):
-            if c in double:
-                p_pass(w, s, z, second[c], False, z == PASSES - 1)
-            p_pass(w, s, z, neg_p[c], z == 0, z == PASSES - 1)
-
-        def front(c, z, engine):
-            g = keep.tile([P, M * PACK], BF16, name=f"grouped{c}_{z}", align_bytes=64)
-            cast(c, z, engine, g[:])
-            w = keep.tile([P, M], U32, name=f"wa_w{c}_{z}", align_bytes=64)
-            s = keep.tile([P, M], U8, name=f"wa_s{c}_{z}", align_bytes=64)
-            nc.vector.quantize_mx(out=w[:].bitcast(FP8X4), scales=s[:], in_=g[:])
-            p_passes(c, z, w[:], s[:])
-
-        def back(c, parts):
-            th = keep.tile([M, J], F32, name=f"th{c}")
-            res = keep.tile([M, J], F32, name=f"res{c}")
-            if c in double:
-                src = second[c]
             else:
-                q_cols = q_sb[:, c * J : (c + 1) * J]
-                nc.scalar.copy(out=q_cols, in_=second[c][:])
-                src = keep.tile([M, J], F32, name=f"diff{c}")
-                nc.vector.tensor_tensor(out=src[:], in0=neg_p[c][:], in1=q_cols, op=ALU.add)
-            w = J // parts
-            for h in range(parts):
-                cols = slice(h * w, (h + 1) * w)
-                nc.scalar.activation(out=th[:, cols], in_=src[:, cols], func=ACT.Tanh, scale=-1.0)
-                nc.vector.tensor_tensor(out=res[:, cols], in0=th[:, cols], in1=neg_p[c][:, cols], op=ALU.subtract)
-                nc.sync.dma_start(out=out[c * M : (c + 1) * M, cols], in_=res[:, cols])
+                nc.vector.tensor_scalar(out=dst, in0=src, scalar1=-1.0, scalar2=None, op0=ALU.mult)
+            codes = keep.tile([P, M], U32, name=f"wa_codes{c}_{z}", align_bytes=64)
+            plane = keep.tile([P, M], U8, name=f"wa_plane{c}_{z}", align_bytes=64)
+            nc.vector.quantize_mx(out=codes[:].bitcast(FP8X4), scales=plane[:], in_=grouped[:])
+            if c in SUMMED_IN_PSUM:
+                against_x(q_bank[c], z, codes[:].bitcast(FP8X4), plane[:], False, z == PASSES - 1)
+            against_x(neg_p[c], z, codes[:].bitcast(FP8X4), plane[:], z == 0, z == PASSES - 1)
 
-        cast_engine = "SSSSSVSV"
+        def finish(c):
+            if c in SUMMED_IN_PSUM:
+                q_less_p = q_bank[c]
+            else:
+                q_copy = keep.tile([M, J], F32, name=f"q_copy{c}")
+                nc.scalar.copy(out=q_copy[:], in_=q_bank[c][:])
+                slot = "grouped2_0" if c == 0 else f"q_less_p{c}"
+                q_less_p = keep.tile([M, J], F32, name=f"q_less_p{c}", tag=slot, align_bytes=64)
+                nc.vector.tensor_tensor(out=q_less_p[:], in0=neg_p[c][:], in1=q_copy[:], op=ALU.add)
+            bent = keep.tile([M, J], F32, name=f"bent{c}")
+            result = keep.tile([M, J], F32, name=f"result{c}")
+            width = J // 2 if c == LAST else J
+            for j0 in range(0, J, width):
+                cols = slice(j0, j0 + width)
+                nc.scalar.activation(out=bent[:, cols], in_=q_less_p[:, cols], func=ACT.Tanh, scale=-1.0)
+                nc.vector.tensor_tensor(out=result[:, cols], in0=bent[:, cols], in1=neg_p[c][:, cols], op=ALU.subtract)
+                nc.sync.dma_start(out=out[c * M : (c + 1) * M, cols], in_=result[:, cols])
 
-        def fronts(c):
-            for z in range(PASSES):
-                front(c, z, cast_engine[PASSES * c + z])
-
+        for z in range(PASSES):
+            for c in range(TILES):
+                q_pass(c, z)
+        for c, z in wa_pieces:
+            p_pass(c, z)
         for c in range(TILES):
-            q_pass(c, 0)
-        q_pass(0, 1)
-        q_pass(1, 1)
-        fronts(0)
-        q_pass(2, 1)
-        q_pass(3, 1)
-        for c in range(1, TILES):
-            fronts(c)
-        q_sb = keep.tile([M, 2 * J], F32, name="q_sb", tag="raw1")
-        for c in range(TILES - 1):
-            back(c, 1)
-        back(3, 2)
+            finish(c)

@@ -25,7 +25,7 @@ TILES = N // M
 PIECE = PACK * M
 QUADS = 4
 SPREAD = 8
-RUN = 2
+RUN = 4
 SUMMED_IN_PSUM = range(TILES // 2, TILES)
 LAST = TILES - 1
 
@@ -44,7 +44,6 @@ def tile_list_expert_contrast_kernel(tc, xq_words, xq_scales, wa, wb_words, wb_s
         x_words = [keep.tile([P, J], U32, name=f"x_words{z}", align_bytes=64) for z in range(PASSES)]
         wb_codes = keep.tile([P, PASSES * 2 * N], U8, name="wb_codes", align_bytes=64)
         wb_planes = keep.tile([P, PASSES * N], U8, name="wb_planes", align_bytes=64)
-        wa_rows = [keep.tile([P, PASSES * PIECE], F32, name=f"wa_rows{c}") for c in range(TILES)]
 
         table_words = x_scale_table[:].bitcast(I32)
         nc.vector.memset(table_words[:, 0 : T // 4], 0)
@@ -76,22 +75,28 @@ def tile_list_expert_contrast_kernel(tc, xq_words, xq_scales, wa, wb_words, wb_s
         for z in range(PASSES):
             nc.vector.tensor_copy(x_words[z][:], x_tables[z][:].bitcast(U32).indirect(offsets[:]))
 
-        def load_wa(c, z):
-            nc.sync.dma_start(
-                out=wa_rows[c][:, z * PIECE : (z + 1) * PIECE].rearrange("p (t n) -> p t n", t=PACK),
-                in_=wa[z * K_PASS : (z + 1) * K_PASS, c * M : (c + 1) * M].rearrange("(p t) n -> p t n", t=PACK),
-            )
-
-        wa_pieces = [(c, z) for c in range(TILES) for z in range(PASSES)]
-        load_wa(*wa_pieces[0])
         for quad in range(QUADS):
-            queue = nc.sync if quad < QUADS // 2 else nc.scalar
-            queue.dma_start(
+            nc.scalar.dma_start(
                 out=x_planes[32 * quad : 32 * quad + 4, :].bitcast(I32),
                 in_=x_scale_picked[32 * quad : 32 * quad + 32 : SPREAD, :].bitcast(I32),
             )
-        for c, z in wa_pieces[1:]:
-            load_wa(c, z)
+
+        wa_rows = {}
+
+        def load_wa(z, tiles):
+            rows = keep.tile([P, PACK, len(tiles) * M], F32, name=f"wa_rows{z}_{tiles[0]}")
+            cols = slice(tiles[0] * M, (tiles[-1] + 1) * M)
+            nc.sync.dma_start(
+                out=rows[:], in_=wa[z * K_PASS : (z + 1) * K_PASS, cols].rearrange("(p t) n -> p t n", t=PACK)
+            )
+            for place, c in enumerate(tiles):
+                wa_rows[c, z] = rows[:, :, place * M : (place + 1) * M]
+
+        load_wa(0, (0, 1))
+        load_wa(1, (0, 1))
+        load_wa(0, (2, 3))
+        load_wa(1, (2,))
+        load_wa(1, (3,))
 
         neg_p = [psum.tile([M, J], F32, name=f"neg_p{c}") for c in range(TILES)]
         q_bank = [psum.tile([M, J], F32, name=f"q_bank{c}") for c in range(TILES)]
@@ -114,10 +119,10 @@ def tile_list_expert_contrast_kernel(tc, xq_words, xq_scales, wa, wb_words, wb_s
             against_x(q_bank[c], z, codes, wb_planes[:, first : first + M], z == 0, closes)
 
         def p_pass(c, z):
-            grouped = keep.tile([P, PIECE], BF16, name=f"grouped{c}_{z}", tag=f"grouped{c}_{z}", align_bytes=64)
-            src = wa_rows[c][:, z * PIECE : (z + 1) * PIECE].rearrange("p (t g i) -> p g t i", t=PACK, i=RUN)
+            grouped = keep.tile([P, PIECE], BF16, name=f"grouped{c}_{z}", align_bytes=64)
+            src = wa_rows[c, z].rearrange("p t (g i) -> p g t i", i=RUN)
             dst = grouped[:].rearrange("p (g i t) -> p g t i", i=RUN, t=PACK)
-            if c == 0 or (c, z) == (LAST, 0):
+            if c in SUMMED_IN_PSUM and z == PASSES - 1:
                 nc.scalar.activation(out=dst, in_=src, func=ACT.Copy, scale=-1.0)
             else:
                 nc.vector.tensor_scalar(out=dst, in0=src, scalar1=-1.0, scalar2=None, op0=ALU.mult)
@@ -134,8 +139,7 @@ def tile_list_expert_contrast_kernel(tc, xq_words, xq_scales, wa, wb_words, wb_s
             else:
                 q_copy = keep.tile([M, J], F32, name=f"q_copy{c}")
                 nc.scalar.copy(out=q_copy[:], in_=q_bank[c][:])
-                slot = "grouped2_0" if c == 0 else f"q_less_p{c}"
-                q_less_p = keep.tile([M, J], F32, name=f"q_less_p{c}", tag=slot, align_bytes=64)
+                q_less_p = keep.tile([M, J], F32, name=f"q_less_p{c}")
                 nc.vector.tensor_tensor(out=q_less_p[:], in0=neg_p[c][:], in1=q_copy[:], op=ALU.add)
             bent = keep.tile([M, J], F32, name=f"bent{c}")
             result = keep.tile([M, J], F32, name=f"result{c}")
@@ -149,7 +153,8 @@ def tile_list_expert_contrast_kernel(tc, xq_words, xq_scales, wa, wb_words, wb_s
         for z in range(PASSES):
             for c in range(TILES):
                 q_pass(c, z)
-        for c, z in wa_pieces:
-            p_pass(c, z)
+        for c in range(TILES):
+            for z in range(PASSES):
+                p_pass(c, z)
         for c in range(TILES):
             finish(c)

from contextlib import ExitStack

import concourse.mybir as mybir

K, T, J, N = 1024, 2048, 512, 512
FLOPS = 2 * 2 * K * N * J

F32 = mybir.dt.float32
BF16 = mybir.dt.bfloat16
I32 = mybir.dt.int32
U32 = mybir.dt.uint32
U16 = mybir.dt.uint16
U8 = mybir.dt.uint8
FP8X4 = mybir.dt.float8_e4m3fn_x4
FP4X4 = mybir.dt.float4_e2m1fn_x4
ALU = mybir.AluOpType
ACT = mybir.ActivationFunctionType

P = 128
PACK = 4
K_PASS = P * PACK
PASSES = K // K_PASS
M = 128
TILES = N // M
PIECE = PACK * M
QUADS = 4
SPREAD = 8
RUN = 4
SUMMED_IN_PSUM = range(TILES // 2, TILES)
LAST = TILES - 1


def tile_list_expert_contrast_kernel(tc, xq_words, xq_scales, wa, wb_words, wb_scales, offs, out):
    nc = tc.nc
    with ExitStack() as ctx:
        keep = ctx.enter_context(tc.tile_pool(name="keep", bufs=1))
        psum = ctx.enter_context(tc.psum_pool(name="psum", bufs=1))

        offsets = keep.tile([P, J // 16], U16, name="offsets")
        x_scale_table = keep.tile([P, PASSES * T], U8, name="x_scale_table", align_bytes=64)
        x_scale_picked = keep.tile([P, PASSES * J], U8, name="x_scale_picked", align_bytes=64)
        x_planes = keep.tile([P, PASSES * J], U8, name="x_planes", align_bytes=64)
        x_tables = [keep.tile([P, T], I32, name=f"x_table{z}", align_bytes=64) for z in range(PASSES)]
        x_words = [keep.tile([P, J], U32, name=f"x_words{z}", align_bytes=64) for z in range(PASSES)]
        wb_codes = keep.tile([P, PASSES * 2 * N], U8, name="wb_codes", align_bytes=64)
        wb_planes = keep.tile([P, PASSES * N], U8, name="wb_planes", align_bytes=64)

        table_words = x_scale_table[:].bitcast(I32)
        nc.vector.memset(table_words[:, 0 : T // 4], 0)
        nc.gpsimd.memset(table_words[:, T // 4 : T // 2], 0)
        nc.vector.memset(wb_planes[:].bitcast(I32), 0)
        nc.vector.memset(x_planes[:].bitcast(I32), 0)

        nc.sync.dma_start(offsets[:], offs)
        nc.sync.dma_start(
            out=x_scale_table[0:P:SPREAD, :].bitcast(I32).rearrange("b (z c) -> b z c", z=PASSES),
            in_=xq_scales.bitcast(I32).rearrange("z b c -> b z c"),
        )
        nc.sync.dma_start(
            out=wb_codes[:].bitcast(I32).rearrange("p (z c) -> p z c", z=PASSES),
            in_=wb_words.bitcast(I32).rearrange("z p c -> p z c"),
        )
        for z in range(PASSES):
            nc.sync.dma_start(out=x_tables[z][:], in_=xq_words[z].rearrange("p c r -> p (c r)").bitcast(I32))
        for quad in range(QUADS):
            nc.scalar.dma_start(
                out=wb_planes[32 * quad : 32 * quad + 4, :].bitcast(I32).rearrange("r (z c) -> r z c", z=PASSES),
                in_=wb_scales[:, 4 * quad : 4 * quad + 4, :].bitcast(I32).rearrange("z r c -> r z c"),
            )

        for z in range(PASSES):
            nc.vector.tensor_copy(
                x_scale_picked[:, z * J : (z + 1) * J], x_scale_table[:, z * T : (z + 1) * T].indirect(offsets[:])
            )
        for z in range(PASSES):
            nc.vector.tensor_copy(x_words[z][:], x_tables[z][:].bitcast(U32).indirect(offsets[:]))

        for quad in range(QUADS):
            nc.scalar.dma_start(
                out=x_planes[32 * quad : 32 * quad + 4, :].bitcast(I32),
                in_=x_scale_picked[32 * quad : 32 * quad + 32 : SPREAD, :].bitcast(I32),
            )

        wa_rows = {}

        def load_wa(z, tiles):
            rows = keep.tile([P, PACK, len(tiles) * M], F32, name=f"wa_rows{z}_{tiles[0]}")
            cols = slice(tiles[0] * M, (tiles[-1] + 1) * M)
            nc.sync.dma_start(
                out=rows[:], in_=wa[z * K_PASS : (z + 1) * K_PASS, cols].rearrange("(p t) n -> p t n", t=PACK)
            )
            for place, c in enumerate(tiles):
                wa_rows[c, z] = rows[:, :, place * M : (place + 1) * M]

        load_wa(0, (0, 1))
        load_wa(1, (0, 1))
        load_wa(0, (2, 3))
        load_wa(1, (2,))
        load_wa(1, (3,))

        neg_p = [psum.tile([M, J], F32, name=f"neg_p{c}") for c in range(TILES)]
        q_bank = [psum.tile([M, J], F32, name=f"q_bank{c}") for c in range(TILES)]

        def against_x(bank, z, codes, plane, start, stop):
            nc.tensor.matmul_mx(
                out=bank[:],
                lhsT=codes,
                lhsT_scale=plane,
                rhs=x_words[z][:].bitcast(FP8X4),
                rhs_scale=x_planes[:, z * J : (z + 1) * J],
                start=start,
                stop=stop,
            )

        def q_pass(c, z):
            first = z * N + c * M
            closes = z == PASSES - 1 and c not in SUMMED_IN_PSUM
            codes = wb_codes[:, 2 * first : 2 * (first + M)].bitcast(FP4X4)
            against_x(q_bank[c], z, codes, wb_planes[:, first : first + M], z == 0, closes)

        def p_pass(c, z):
            grouped = keep.tile([P, PIECE], BF16, name=f"grouped{c}_{z}", align_bytes=64)
            src = wa_rows[c, z].rearrange("p t (g i) -> p g t i", i=RUN)
            dst = grouped[:].rearrange("p (g i t) -> p g t i", i=RUN, t=PACK)
            if c in SUMMED_IN_PSUM and z == PASSES - 1:
                nc.scalar.activation(out=dst, in_=src, func=ACT.Copy, scale=-1.0)
            else:
                nc.vector.tensor_scalar(out=dst, in0=src, scalar1=-1.0, scalar2=None, op0=ALU.mult)
            codes = keep.tile([P, M], U32, name=f"wa_codes{c}_{z}", align_bytes=64)
            plane = keep.tile([P, M], U8, name=f"wa_plane{c}_{z}", align_bytes=64)
            nc.vector.quantize_mx(out=codes[:].bitcast(FP8X4), scales=plane[:], in_=grouped[:])
            if c in SUMMED_IN_PSUM:
                against_x(q_bank[c], z, codes[:].bitcast(FP8X4), plane[:], False, z == PASSES - 1)
            against_x(neg_p[c], z, codes[:].bitcast(FP8X4), plane[:], z == 0, z == PASSES - 1)

        def finish(c):
            if c in SUMMED_IN_PSUM:
                q_less_p = q_bank[c]
            else:
                q_copy = keep.tile([M, J], F32, name=f"q_copy{c}")
                nc.scalar.copy(out=q_copy[:], in_=q_bank[c][:])
                q_less_p = keep.tile([M, J], F32, name=f"q_less_p{c}")
                nc.vector.tensor_tensor(out=q_less_p[:], in0=neg_p[c][:], in1=q_copy[:], op=ALU.add)
            bent = keep.tile([M, J], F32, name=f"bent{c}")
            result = keep.tile([M, J], F32, name=f"result{c}")
            width = J // 2 if c == LAST else J
            for j0 in range(0, J, width):
                cols = slice(j0, j0 + width)
                nc.scalar.activation(out=bent[:, cols], in_=q_less_p[:, cols], func=ACT.Tanh, scale=-1.0)
                nc.vector.tensor_tensor(out=result[:, cols], in0=bent[:, cols], in1=neg_p[c][:, cols], op=ALU.subtract)
                nc.sync.dma_start(out=out[c * M : (c + 1) * M, cols], in_=result[:, cols])

        for z in range(PASSES):
            for c in range(TILES):
                q_pass(c, z)
        for c in range(TILES):
            for z in range(PASSES):
                p_pass(c, z)
        for c in range(TILES):
            finish(c)
